import numpy as np
import ml_dtypes


def mxq(x, axis, fmt="e4m3"):
    dtype, down = {"e4m3": (ml_dtypes.float8_e4m3fn, 7), "e5m2": (ml_dtypes.float8_e5m2, 14)}[fmt]
    v = np.moveaxis(np.asarray(x, np.float32).astype(ml_dtypes.bfloat16).astype(np.float64), axis, -1)
    blocks = v.reshape(v.shape[:-1] + (-1, 32))
    amax = np.abs(blocks).max(-1, keepdims=True)
    byte = np.maximum(np.where(amax > 0, np.frexp(amax)[1] - 1 + 127, 0) - down, 1)
    scale = np.exp2(byte - 127.0)
    codes = (blocks / scale).astype(np.float32).astype(dtype).astype(np.float64)
    return np.moveaxis((codes * scale).reshape(v.shape), -1, axis)


WIDE = False


def mx_kscale(k):
    if not WIDE:
        return np.ones(k)
    levels = np.array([10, -10, 5, -5, 0])
    if k % 512:
        return np.exp2(np.random.permutation(np.resize(levels, k // 32))).repeat(32)
    a = np.empty((k // 512, 16))
    for p in range(k // 512):
        a[p, :8] = np.random.permutation(np.resize(levels, 8))
        for g in range(8):
            far = levels[np.abs(levels - a[p, g]) >= 10]
            a[p, g + 8] = far[np.random.randint(len(far))]
    return np.exp2(a.ravel()).repeat(32)


def f64(x):
    return np.asarray(x).astype(np.float64)


def striped(idx):
    return np.tile(np.asarray(idx).reshape(-1, 16).T, (8, 1)).astype(np.uint16)


def unstriped(offs):
    return offs[:16].T.reshape(-1).astype(np.int64)


E2M1 = np.array([0.0, 0.5, 1.0, 1.5, 2.0, 3.0, 4.0, 6.0, -0.0, -0.5, -1.0, -1.5, -2.0, -3.0, -4.0, -6.0])


def pack_weight(w, fmt):
    k, n = w.shape
    w = f64(np.asarray(w, np.float32).astype(ml_dtypes.bfloat16)).reshape(k // 32, 32, n)
    amax = np.abs(w).max(1)
    if fmt == "e4m3":
        byte = np.frexp(amax)[1] - 1 + 127 - 7
    else:
        mant, ex = np.frexp(amax / 6.0)
        byte = np.where(mant > 0.5, ex, ex - 1) + 127
    byte = np.clip(np.where(amax > 0, byte, 1), 1, 254)
    scaled = (w * np.exp2(127.0 - byte)[:, None, :]).reshape(k, n).astype(np.float32)
    by_word = np.ascontiguousarray(scaled.reshape(k // 512, 128, 4, n).transpose(0, 1, 3, 2))
    if fmt == "e4m3":
        words = by_word.astype(ml_dtypes.float8_e4m3fn).view(np.uint8)
    else:
        c = by_word.astype(ml_dtypes.float4_e2m1fn).view(np.uint8) & 0xF
        words = (c[..., 0::2] | (c[..., 1::2] << 4)).reshape(k // 512, 128, 2 * n)
    return np.ascontiguousarray(words), np.ascontiguousarray(byte.astype(np.uint8).reshape(k // 512, 16, n))


def unpack_weight(words, scales, fmt):
    g, _, n = scales.shape
    words = np.ascontiguousarray(words).reshape(g, 128, n, -1)
    if fmt == "e4m3":
        vals = words.view(ml_dtypes.float8_e4m3fn).astype(np.float64)
    else:
        nib = np.empty((g, 128, n, 4), np.uint8)
        nib[..., 0::2] = words & 0xF
        nib[..., 1::2] = words >> 4
        vals = E2M1[nib]
    vals = vals * np.repeat(np.exp2(scales.astype(np.float64) - 127.0), 8, axis=1)[..., None]
    return vals.transpose(0, 1, 3, 2).reshape(g * 512, n)


def sgn(shape):
    return np.random.uniform(0.5, 2.0, shape) * np.where(np.random.standard_normal(shape) < 0, -1.0, 1.0)


K, T, J, R, O, U, E = 512, 1024, 256, 512, 128, 128, 256


def setup_inputs():
    n = np.random.standard_normal
    idx = np.random.permutation(T)[:J]
    idx2 = np.random.permutation(J)[:O]
    idx3 = np.random.permutation(J)[:U]
    idx4 = np.random.permutation(E)[:U]
    fk = mx_kscale(K)
    fr = mx_kscale(R)
    xtp = pack_weight(n((K, T)) / fk[:, None], "e4m3")
    wp = pack_weight(n((K, R)) * 1 / np.sqrt(K) * fk[:, None], "e2m1")
    return {
        "xt_words": xtp[0],
        "xt_scales": xtp[1],
        "w_words": wp[0],
        "w_scales": wp[1],
        "sg": (0.35 * sgn((R, 1))).astype(np.float32),
        "lo": (np.random.uniform(-1.0, 1.0, (R, 1)) + np.log(fr)[:, None]).astype(np.float32),
        "sa": (sgn((R, 1)) / fr[:, None] / np.sqrt(R)).astype(np.float32),
        "so": (np.random.uniform(0.5, 1.6, (O, 1))).astype(np.float32),
        "offs": striped(idx),
        "offs2": striped(idx2),
        "offs3": striped(idx3),
        "offs4": striped(idx4),
    }


def reference(xt_words, xt_scales, w_words, w_scales, sg, lo, sa, so, offs, offs2, offs3, offs4):
    idx = unstriped(offs)
    idx2 = unstriped(offs2)
    idx3 = unstriped(offs3)
    idx4 = unstriped(offs4)
    xtu = unpack_weight(xt_words, xt_scales, "e4m3")
    wu = unpack_weight(w_words, w_scales, "e2m1")
    xtidxg = xtu[:, idx]
    a = wu.T @ xtidxg
    z1 = np.exp(a[:, idx2] * f64(sg) + f64(lo))
    z2 = a[:, idx3] * f64(sa)
    z1q = mxq(z1, 0, "e4m3")
    z2q = mxq(z2, 0, "e4m3")
    p = z1q.T @ z2q
    y = np.zeros((O, E))
    y[:, idx4] = p * f64(so)
    return y

@@ -1,0 +1,153 @@
+from contextlib import ExitStack
+
+import concourse.mybir as mybir
+
+K, T, J, R, O, U, E = 512, 1024, 256, 512, 128, 128, 256
+FLOPS = 2 * K * R * J + 2 * R * O * U
+
+F32 = mybir.dt.float32
+BF16 = mybir.dt.bfloat16
+I32 = mybir.dt.int32
+U32 = mybir.dt.uint32
+U16 = mybir.dt.uint16
+U8 = mybir.dt.uint8
+FP8X4 = mybir.dt.float8_e4m3fn_x4
+FP4X4 = mybir.dt.float4_e2m1fn_x4
+ACT = mybir.ActivationFunctionType
+
+P = 128
+PACK = 4
+
+
+def tile_list_selfenergies_kernel(tc, xt_words, xt_scales, w_words, w_scales, sg, lo, sa, so, offs, offs2, offs3, offs4, out):
+    nc = tc.nc
+    with ExitStack() as ctx:
+        keep = ctx.enter_context(tc.tile_pool(name="keep", bufs=1))
+        psum = ctx.enter_context(tc.psum_pool(name="psum", bufs=1))
+
+        idx1 = keep.tile([P, J // 16], U16)
+        idx2 = keep.tile([P, O // 16], U16)
+        idx3 = keep.tile([P, U // 16], U16)
+        idx4 = keep.tile([P, U // 16], U16)
+        x_words = keep.tile([P, T], I32, align_bytes=64)
+        x_scale = keep.tile([P, T], U8, align_bytes=64)
+        w_raw = keep.tile([P, 2 * R], U8, align_bytes=64)
+        ws_rows = keep.tile([4, 4, R // 4], I32, align_bytes=64)
+        ws_raw = keep.tile([P, R], U8, align_bytes=64)
+        sg_t = keep.tile([P, PACK], F32, align_bytes=64, tag="z2_1")
+        lo_t = keep.tile([P, PACK], F32)
+        sa_t = keep.tile([P, PACK], F32)
+        so_t = keep.tile([P, 1], F32)
+
+        nc.vector.memset(x_scale[:].bitcast(I32), 0)
+        nc.scalar.dma_start(ws_rows[:], w_scales[0].bitcast(I32).rearrange("(q r) c -> r q c", r=4))
+        nc.sync.dma_start(idx1[:], offs)
+        nc.scalar.dma_start(x_words[:], xt_words[0].rearrange("p n t -> p (n t)").bitcast(I32))
+        xs_rows = xt_scales[0].bitcast(I32)
+        for r in range(4):
+            nc.sync.dma_start(x_scale[r:P:32, :].bitcast(I32), xs_rows[r:16:4, :])
+        nc.scalar.dma_start(w_raw[:].bitcast(I32), w_words[0].bitcast(I32))
+        nc.gpsimd.dma_start(sg_t[:], sg.rearrange("(p t) o -> p (t o)", t=PACK))
+        nc.gpsimd.dma_start(lo_t[:], lo.rearrange("(p t) o -> p (t o)", t=PACK))
+        nc.sync.dma_start(idx2[:], offs2)
+        nc.sync.dma_start(idx3[:], offs3)
+        nc.sync.dma_start(sa_t[:], sa.rearrange("(p t) o -> p (t o)", t=PACK))
+        nc.sync.dma_start(idx4[:], offs4)
+        nc.sync.dma_start(so_t[:], so)
+
+        nc.vector.memset(ws_raw[:].bitcast(I32), 0)
+        page = keep.tile([P, E], F32)
+        nc.vector.memset(page[:], 0.0)
+
+        w_dealt = keep.tile([P, 2 * R], U8, align_bytes=64)
+        ws_dealt = keep.tile([P, R], U8, align_bytes=64)
+        w_by_t = w_raw[:].bitcast(U16).rearrange("p (m t) -> p t m", t=PACK)
+        w_out = w_dealt[:].bitcast(U16).rearrange("p (t m) -> p t m", t=PACK)
+        nc.scalar.copy(out=w_out[:, 0, :], in_=w_by_t[:, 0, :])
+        nc.scalar.copy(out=w_out[:, 1:PACK, :], in_=w_by_t[:, 1:PACK, :])
+        xg_scale = keep.tile([P, J], U8, align_bytes=64)
+        xg_words = keep.tile([P, J], U32, align_bytes=64)
+        for q in range(4):
+            nc.vector.tensor_copy(ws_raw[32 * q : 32 * q + 4, :].bitcast(I32), ws_rows[:, q, :])
+        ws_by_t = ws_raw[:].rearrange("p (m t) -> p t m", t=PACK)
+        nc.vector.tensor_copy(out=ws_dealt[:, 0:P], in_=ws_by_t[:, 0, :])
+        nc.vector.tensor_copy(xg_scale[:], x_scale[:].indirect(idx1[:]))
+        HJ = J // 2
+        for h in range(2):
+            nc.vector.tensor_copy(
+                xg_words[:, h * HJ : (h + 1) * HJ],
+                x_words[:].bitcast(U32).indirect(idx1[:, h * HJ // 16 : (h + 1) * HJ // 16]),
+            )
+        nc.vector.tensor_copy(out=ws_dealt[:, P:R].rearrange("p (t m) -> p t m", t=PACK - 1), in_=ws_by_t[:, 1:PACK, :])
+
+        def hidden(acc, t, cols):
+            nc.tensor.matmul_mx(
+                out=acc[:],
+                lhsT=w_dealt[:, 2 * P * t : 2 * P * (t + 1)].bitcast(FP4X4),
+                lhsT_scale=ws_dealt[:, P * t : P * (t + 1)],
+                rhs=xg_words[:, cols].bitcast(FP8X4),
+                rhs_scale=xg_scale[:, cols],
+                start=True,
+                stop=True,
+            )
+
+        a_rows = [keep.tile([P, J], F32, name="a%d" % t) for t in range(PACK)]
+        acc_lo = psum.tile([P, HJ], F32)
+        acc_hi = psum.tile([P, HJ], F32)
+        hidden(acc_lo, 0, slice(0, HJ))
+        hidden(acc_hi, 0, slice(HJ, J))
+        nc.scalar.copy(out=a_rows[0][:, 0:HJ], in_=acc_lo[:])
+        nc.vector.tensor_copy(a_rows[0][:, HJ:J], acc_hi[:])
+        for t in range(1, PACK):
+            acc = psum.tile([P, J], F32, name="acc%d" % t)
+            hidden(acc, t, slice(0, J))
+            nc.vector.tensor_copy(a_rows[t][:], acc[:])
+
+        z1 = keep.tile([P, PACK * O], BF16, align_bytes=64)
+        for t in range(PACK):
+            nc.scalar.activation(
+                out=z1[:, t : PACK * O : PACK],
+                in_=a_rows[t][:].indirect(idx2[:]),
+                func=ACT.Exp,
+                bias=lo_t[:, t : t + 1],
+                scale=sg_t[:, t : t + 1],
+            )
+        z1_codes = keep.tile([P, O], U32, align_bytes=64)
+        z1_scale = keep.tile([P, O], U8, align_bytes=64)
+        nc.vector.quantize_mx(out=z1_codes[:].bitcast(FP8X4), scales=z1_scale[:], in_=z1[:])
+
+        HU = U // 2
+        p_rows = []
+        for h in range(2):
+            z2 = keep.tile([P, PACK * HU], BF16, align_bytes=64, name="z2_%d" % h, tag="z2_%d" % h)
+            for t in range(PACK):
+                nc.scalar.activation(
+                    out=z2[:, t : PACK * HU : PACK],
+                    in_=a_rows[t][:].indirect(idx3[:, h * HU // 16 : (h + 1) * HU // 16]),
+                    func=ACT.Copy,
+                    scale=sa_t[:, t : t + 1],
+                )
+            z2_codes = keep.tile([P, HU], U32, align_bytes=64, name="z2_codes%d" % h)
+            z2_scale = keep.tile([P, HU], U8, align_bytes=64, name="z2_scale%d" % h)
+            nc.vector.quantize_mx(out=z2_codes[:].bitcast(FP8X4), scales=z2_scale[:], in_=z2[:])
+            p_acc = psum.tile([P, HU], F32, name="p_acc%d" % h)
+            nc.tensor.matmul_mx(
+                out=p_acc[:],
+                lhsT=z1_codes[:].bitcast(FP8X4),
+                lhsT_scale=z1_scale[:],
+                rhs=z2_codes[:].bitcast(FP8X4),
+                rhs_scale=z2_scale[:],
+                start=True,
+                stop=True,
+            )
+            p_sb = keep.tile([P, HU], F32, name="p_sb%d" % h)
+            nc.vector.tensor_copy(p_sb[:], p_acc[:])
+            p_rows.append(p_sb)
+        for h in range(2):
+            nc.scalar.activation(
+                out=page[:].indirect(idx4[:, h * HU // 16 : (h + 1) * HU // 16]),
+                in_=p_rows[h][:],
+                func=ACT.Copy,
+                scale=so_t[:],
+            )
+        nc.sync.dma_start(out, page[:])

@@ -40,16 +40,17 @@ def tile_list_selfenergies_kernel(tc, xt_words, xt_scales, w_words, w_scales, sg
         so_t = keep.tile([P, 1], F32)
 
         nc.vector.memset(x_scale[:].bitcast(I32), 0)
-        nc.scalar.dma_start(ws_rows[:], w_scales[0].bitcast(I32).rearrange("(q r) c -> r q c", r=4))
         nc.sync.dma_start(idx1[:], offs)
-        nc.scalar.dma_start(x_words[:], xt_words[0].rearrange("p n t -> p (n t)").bitcast(I32))
+        nc.scalar.dma_start(w_raw[:].bitcast(I32), w_words[0].bitcast(I32))
+        nc.sync.dma_start(ws_rows[:], w_scales[0].bitcast(I32).rearrange("(q r) c -> r q c", r=4))
         xs_rows = xt_scales[0].bitcast(I32)
         for r in range(4):
-            nc.sync.dma_start(x_scale[r:P:32, :].bitcast(I32), xs_rows[r:16:4, :])
-        nc.scalar.dma_start(w_raw[:].bitcast(I32), w_words[0].bitcast(I32))
-        nc.gpsimd.dma_start(sg_t[:], sg.rearrange("(p t) o -> p (t o)", t=PACK))
-        nc.gpsimd.dma_start(lo_t[:], lo.rearrange("(p t) o -> p (t o)", t=PACK))
+            queue = nc.sync if r < 2 else nc.scalar
+            queue.dma_start(x_scale[r:P:32, :].bitcast(I32), xs_rows[r:16:4, :])
+        nc.sync.dma_start(x_words[:], xt_words[0].rearrange("p n t -> p (n t)").bitcast(I32))
         nc.sync.dma_start(idx2[:], offs2)
+        nc.sync.dma_start(sg_t[:], sg.rearrange("(p t) o -> p (t o)", t=PACK))
+        nc.sync.dma_start(lo_t[:], lo.rearrange("(p t) o -> p (t o)", t=PACK))
         nc.sync.dma_start(idx3[:], offs3)
         nc.sync.dma_start(sa_t[:], sa.rearrange("(p t) o -> p (t o)", t=PACK))
         nc.sync.dma_start(idx4[:], offs4)
@@ -63,14 +64,13 @@ def tile_list_selfenergies_kernel(tc, xt_words, xt_scales, w_words, w_scales, sg
         ws_dealt = keep.tile([P, R], U8, align_bytes=64)
         w_by_t = w_raw[:].bitcast(U16).rearrange("p (m t) -> p t m", t=PACK)
         w_out = w_dealt[:].bitcast(U16).rearrange("p (t m) -> p t m", t=PACK)
-        nc.scalar.copy(out=w_out[:, 0, :], in_=w_by_t[:, 0, :])
-        nc.scalar.copy(out=w_out[:, 1:PACK, :], in_=w_by_t[:, 1:PACK, :])
+        nc.scalar.copy(out=w_out, in_=w_by_t)
         xg_scale = keep.tile([P, J], U8, align_bytes=64)
         xg_words = keep.tile([P, J], U32, align_bytes=64)
         for q in range(4):
             nc.vector.tensor_copy(ws_raw[32 * q : 32 * q + 4, :].bitcast(I32), ws_rows[:, q, :])
         ws_by_t = ws_raw[:].rearrange("p (m t) -> p t m", t=PACK)
-        nc.vector.tensor_copy(out=ws_dealt[:, 0:P], in_=ws_by_t[:, 0, :])
+        nc.gpsimd.tensor_copy(out=ws_dealt[:, 0:P], in_=ws_by_t[:, 0, :])
         nc.vector.tensor_copy(xg_scale[:], x_scale[:].indirect(idx1[:]))
         HJ = J // 2
         for h in range(2):
@@ -78,7 +78,7 @@ def tile_list_selfenergies_kernel(tc, xt_words, xt_scales, w_words, w_scales, sg
                 xg_words[:, h * HJ : (h + 1) * HJ],
                 x_words[:].bitcast(U32).indirect(idx1[:, h * HJ // 16 : (h + 1) * HJ // 16]),
             )
-        nc.vector.tensor_copy(out=ws_dealt[:, P:R].rearrange("p (t m) -> p t m", t=PACK - 1), in_=ws_by_t[:, 1:PACK, :])
+        nc.gpsimd.tensor_copy(out=ws_dealt[:, P:R].rearrange("p (t m) -> p t m", t=PACK - 1), in_=ws_by_t[:, 1:PACK, :])
 
         def hidden(acc, t, cols):
             nc.tensor.matmul_mx(

from contextlib import ExitStack

import concourse.mybir as mybir

K, T, J, R, O, U, E = 512, 1024, 256, 512, 128, 128, 256
FLOPS = 2 * K * R * J + 2 * R * O * U

F32 = mybir.dt.float32
BF16 = mybir.dt.bfloat16
I32 = mybir.dt.int32
U32 = mybir.dt.uint32
U16 = mybir.dt.uint16
U8 = mybir.dt.uint8
FP8X4 = mybir.dt.float8_e4m3fn_x4
FP4X4 = mybir.dt.float4_e2m1fn_x4
ACT = mybir.ActivationFunctionType

P = 128
PACK = 4


def tile_list_selfenergies_kernel(tc, xt_words, xt_scales, w_words, w_scales, sg, lo, sa, so, offs, offs2, offs3, offs4, out):
    nc = tc.nc
    with ExitStack() as ctx:
        keep = ctx.enter_context(tc.tile_pool(name="keep", bufs=1))
        psum = ctx.enter_context(tc.psum_pool(name="psum", bufs=1))

        idx1 = keep.tile([P, J // 16], U16)
        idx2 = keep.tile([P, O // 16], U16)
        idx3 = keep.tile([P, U // 16], U16)
        idx4 = keep.tile([P, U // 16], U16)
        x_words = keep.tile([P, T], I32, align_bytes=64)
        x_scale = keep.tile([P, T], U8, align_bytes=64)
        w_raw = keep.tile([P, 2 * R], U8, align_bytes=64)
        ws_rows = keep.tile([4, 4, R // 4], I32, align_bytes=64)
        ws_raw = keep.tile([P, R], U8, align_bytes=64)
        sg_t = keep.tile([P, PACK], F32, align_bytes=64, tag="z2_1")
        lo_t = keep.tile([P, PACK], F32)
        sa_t = keep.tile([P, PACK], F32)
        so_t = keep.tile([P, 1], F32)

        nc.vector.memset(x_scale[:].bitcast(I32), 0)
        nc.sync.dma_start(idx1[:], offs)
        nc.scalar.dma_start(w_raw[:].bitcast(I32), w_words[0].bitcast(I32))
        nc.sync.dma_start(ws_rows[:], w_scales[0].bitcast(I32).rearrange("(q r) c -> r q c", r=4))
        xs_rows = xt_scales[0].bitcast(I32)
        for r in range(4):
            queue = nc.sync if r < 2 else nc.scalar
            queue.dma_start(x_scale[r:P:32, :].bitcast(I32), xs_rows[r:16:4, :])
        nc.sync.dma_start(x_words[:], xt_words[0].rearrange("p n t -> p (n t)").bitcast(I32))
        nc.sync.dma_start(idx2[:], offs2)
        nc.sync.dma_start(sg_t[:], sg.rearrange("(p t) o -> p (t o)", t=PACK))
        nc.sync.dma_start(lo_t[:], lo.rearrange("(p t) o -> p (t o)", t=PACK))
        nc.sync.dma_start(idx3[:], offs3)
        nc.sync.dma_start(sa_t[:], sa.rearrange("(p t) o -> p (t o)", t=PACK))
        nc.sync.dma_start(idx4[:], offs4)
        nc.sync.dma_start(so_t[:], so)

        nc.vector.memset(ws_raw[:].bitcast(I32), 0)
        page = keep.tile([P, E], F32)
        nc.vector.memset(page[:], 0.0)

        w_dealt = keep.tile([P, 2 * R], U8, align_bytes=64)
        ws_dealt = keep.tile([P, R], U8, align_bytes=64)
        w_by_t = w_raw[:].bitcast(U16).rearrange("p (m t) -> p t m", t=PACK)
        w_out = w_dealt[:].bitcast(U16).rearrange("p (t m) -> p t m", t=PACK)
        nc.scalar.copy(out=w_out, in_=w_by_t)
        xg_scale = keep.tile([P, J], U8, align_bytes=64)
        xg_words = keep.tile([P, J], U32, align_bytes=64)
        for q in range(4):
            nc.vector.tensor_copy(ws_raw[32 * q : 32 * q + 4, :].bitcast(I32), ws_rows[:, q, :])
        ws_by_t = ws_raw[:].rearrange("p (m t) -> p t m", t=PACK)
        nc.gpsimd.tensor_copy(out=ws_dealt[:, 0:P], in_=ws_by_t[:, 0, :])
        nc.vector.tensor_copy(xg_scale[:], x_scale[:].indirect(idx1[:]))
        HJ = J // 2
        for h in range(2):
            nc.vector.tensor_copy(
                xg_words[:, h * HJ : (h + 1) * HJ],
                x_words[:].bitcast(U32).indirect(idx1[:, h * HJ // 16 : (h + 1) * HJ // 16]),
            )
        nc.gpsimd.tensor_copy(out=ws_dealt[:, P:R].rearrange("p (t m) -> p t m", t=PACK - 1), in_=ws_by_t[:, 1:PACK, :])

        def hidden(acc, t, cols):
            nc.tensor.matmul_mx(
                out=acc[:],
                lhsT=w_dealt[:, 2 * P * t : 2 * P * (t + 1)].bitcast(FP4X4),
                lhsT_scale=ws_dealt[:, P * t : P * (t + 1)],
                rhs=xg_words[:, cols].bitcast(FP8X4),
                rhs_scale=xg_scale[:, cols],
                start=True,
                stop=True,
            )

        a_rows = [keep.tile([P, J], F32, name="a%d" % t) for t in range(PACK)]
        acc_lo = psum.tile([P, HJ], F32)
        acc_hi = psum.tile([P, HJ], F32)
        hidden(acc_lo, 0, slice(0, HJ))
        hidden(acc_hi, 0, slice(HJ, J))
        nc.scalar.copy(out=a_rows[0][:, 0:HJ], in_=acc_lo[:])
        nc.vector.tensor_copy(a_rows[0][:, HJ:J], acc_hi[:])
        for t in range(1, PACK):
            acc = psum.tile([P, J], F32, name="acc%d" % t)
            hidden(acc, t, slice(0, J))
            nc.vector.tensor_copy(a_rows[t][:], acc[:])

        z1 = keep.tile([P, PACK * O], BF16, align_bytes=64)
        for t in range(PACK):
            nc.scalar.activation(
                out=z1[:, t : PACK * O : PACK],
                in_=a_rows[t][:].indirect(idx2[:]),
                func=ACT.Exp,
                bias=lo_t[:, t : t + 1],
                scale=sg_t[:, t : t + 1],
            )
        z1_codes = keep.tile([P, O], U32, align_bytes=64)
        z1_scale = keep.tile([P, O], U8, align_bytes=64)
        nc.vector.quantize_mx(out=z1_codes[:].bitcast(FP8X4), scales=z1_scale[:], in_=z1[:])

        HU = U // 2
        p_rows = []
        for h in range(2):
            z2 = keep.tile([P, PACK * HU], BF16, align_bytes=64, name="z2_%d" % h, tag="z2_%d" % h)
            for t in range(PACK):
                nc.scalar.activation(
                    out=z2[:, t : PACK * HU : PACK],
                    in_=a_rows[t][:].indirect(idx3[:, h * HU // 16 : (h + 1) * HU // 16]),
                    func=ACT.Copy,
                    scale=sa_t[:, t : t + 1],
                )
            z2_codes = keep.tile([P, HU], U32, align_bytes=64, name="z2_codes%d" % h)
            z2_scale = keep.tile([P, HU], U8, align_bytes=64, name="z2_scale%d" % h)
            nc.vector.quantize_mx(out=z2_codes[:].bitcast(FP8X4), scales=z2_scale[:], in_=z2[:])
            p_acc = psum.tile([P, HU], F32, name="p_acc%d" % h)
            nc.tensor.matmul_mx(
                out=p_acc[:],
                lhsT=z1_codes[:].bitcast(FP8X4),
                lhsT_scale=z1_scale[:],
                rhs=z2_codes[:].bitcast(FP8X4),
                rhs_scale=z2_scale[:],
                start=True,
                stop=True,
            )
            p_sb = keep.tile([P, HU], F32, name="p_sb%d" % h)
            nc.vector.tensor_copy(p_sb[:], p_acc[:])
            p_rows.append(p_sb)
        for h in range(2):
            nc.scalar.activation(
                out=page[:].indirect(idx4[:, h * HU // 16 : (h + 1) * HU // 16]),
                in_=p_rows[h][:],
                func=ACT.Copy,
                scale=so_t[:],
            )
        nc.sync.dma_start(out, page[:])
